import numpy as np
import ml_dtypes


def mxq(x, axis, fmt="e4m3"):
    dtype, down = {"e4m3": (ml_dtypes.float8_e4m3fn, 7), "e5m2": (ml_dtypes.float8_e5m2, 14)}[fmt]
    v = np.moveaxis(np.asarray(x, np.float32).astype(ml_dtypes.bfloat16).astype(np.float64), axis, -1)
    blocks = v.reshape(v.shape[:-1] + (-1, 32))
    amax = np.abs(blocks).max(-1, keepdims=True)
    byte = np.maximum(np.where(amax > 0, np.frexp(amax)[1] - 1 + 127, 0) - down, 1)
    scale = np.exp2(byte - 127.0)
    codes = (blocks / scale).astype(np.float32).astype(dtype).astype(np.float64)
    return np.moveaxis((codes * scale).reshape(v.shape), -1, axis)


WIDE = False


def mx_kscale(k):
    if not WIDE:
        return np.ones(k)
    levels = np.array([10, -10, 5, -5, 0])
    if k % 512:
        return np.exp2(np.random.permutation(np.resize(levels, k // 32))).repeat(32)
    a = np.empty((k // 512, 16))
    for p in range(k // 512):
        a[p, :8] = np.random.permutation(np.resize(levels, 8))
        for g in range(8):
            far = levels[np.abs(levels - a[p, g]) >= 10]
            a[p, g + 8] = far[np.random.randint(len(far))]
    return np.exp2(a.ravel()).repeat(32)


def f64(x):
    return np.asarray(x).astype(np.float64)


def striped(idx):
    return np.tile(idx.reshape(-1, 16).T, (8, 1)).astype(np.uint16)


def unstriped(offs):
    return offs[:16].T.reshape(-1).astype(np.int64)


def pack_weight(w):
    k, n = w.shape
    w = f64(np.asarray(w, np.float32).astype(ml_dtypes.bfloat16)).reshape(k // 32, 32, n)
    amax = np.abs(w).max(1)
    byte = np.clip(np.where(amax > 0, np.frexp(amax)[1] - 1 + 127 - 7, 1), 1, 254)
    scaled = (w * np.exp2(127.0 - byte)[:, None, :]).reshape(k, n).astype(np.float32)
    words = np.ascontiguousarray(scaled.reshape(k // 512, 128, 4, n).transpose(0, 1, 3, 2)).astype(ml_dtypes.float8_e4m3fn).view(np.uint8)
    return words, np.ascontiguousarray(byte.astype(np.uint8).reshape(k // 512, 16, n))


def unpack_weight(words, scales):
    g, p, n, _ = words.shape
    vals = np.ascontiguousarray(words).view(ml_dtypes.float8_e4m3fn).astype(np.float64) * np.repeat(np.exp2(scales.astype(np.float64) - 127.0), 8, axis=1)[..., None]
    return vals.transpose(0, 1, 3, 2).reshape(g * 512, n)


K, T, S, D, N, H, V, U = 512, 2048, 1024, 4, 256, 512, 256, 512


def setup_inputs():
    n = np.random.standard_normal
    s = mx_kscale(K)[:, None]
    u = mx_kscale(H)
    packed_xT = pack_weight(n((K, T)) * s)
    return {
        "x_words": packed_xT[0],
        "x_scales": packed_xT[1],
        "hT": (n((K, H)) / np.sqrt(K) / s).astype(np.float32),
        "imp": (np.random.uniform(0.5, 1.5, (H, U))).astype(np.float32),
        "unit": (np.random.uniform(0.6, 1.4, (H, 1)) * u[:, None]).astype(np.float32),
        "w1": (n((H, N)) / np.sqrt(H) / u[:, None]).astype(np.float32),
        "offs": striped(np.random.permutation(T)[:S]),
        "wl": striped(np.random.permutation(np.concatenate([np.arange(V), np.random.randint(0, V, U - V)]))),
    }


def reference(x_words, x_scales, hT, imp, unit, w1, offs, wl):
    hTq = mxq(f64(hT), 0, "e4m3")
    xq = unpack_weight(x_words, x_scales)[:, unstriped(offs)]
    y = hTq.T @ xq
    mean_ = y.reshape(len(y), -1, D).mean(axis=2)
    dev = y - np.repeat(mean_, D, axis=1)
    r3 = dev * ((dev) ** 2)
    r2 = (dev) ** 2
    sd = np.sqrt(r2.reshape(len(r2), -1, D).mean(axis=2) + 0.1)
    skw = (r3.reshape(len(r3), -1, D).mean(axis=2)) / ((sd) ** 2 + 0.2)
    kw = skw[:, unstriped(wl)]
    sw = sd[:, unstriped(wl)]
    hid = f64(unit) * (kw * f64(imp) + sw)
    return mxq(f64(w1), 0, "e4m3").T @ mxq(hid, 0, "e4m3")

@@ -1,0 +1,191 @@
+from contextlib import ExitStack
+
+import concourse.mybir as mybir
+
+K, T, S, D, N, H, V, U = 512, 2048, 1024, 4, 256, 512, 256, 512
+FLOPS = 2 * K * H * S + 2 * H * N * U
+
+F32 = mybir.dt.float32
+BF16 = mybir.dt.bfloat16
+I32 = mybir.dt.int32
+U32 = mybir.dt.uint32
+U16 = mybir.dt.uint16
+U8 = mybir.dt.uint8
+FP8X4 = mybir.dt.float8_e4m3fn_x4
+ALU = mybir.AluOpType
+ACT = mybir.ActivationFunctionType
+
+P = 128
+PACK = 4
+BANK = 512
+VB = BANK // D
+HALF = U // 2
+
+
+def tile_picked_yvladx_lin_p_kernel(tc, x_words, x_scales, hT, imp, unit, w1, offs, wl, out):
+    nc = tc.nc
+    with ExitStack() as ctx:
+        keep = ctx.enter_context(tc.tile_pool(name="keep", bufs=1))
+        psum = ctx.enter_context(tc.psum_pool(name="psum", bufs=8))
+
+        offs_sb = keep.tile([P, S // 16], U16, name="offs_sb")
+        wl_sb = keep.tile([P, U // 16], U16, name="wl_sb")
+        x_table = keep.tile([P, T], U32, name="x_table", tag="table_then_imp", align_bytes=64)
+        x_scale_table = keep.tile([P, T], U8, name="x_scale_table", tag="scales_then_w", align_bytes=64)
+        h_raw = keep.tile([P, PACK, H], F32, name="h_raw")
+        unit_sb = keep.tile([P, PACK], F32, name="unit_sb")
+
+        nc.vector.memset(x_scale_table[:].bitcast(I32), 0)
+        nc.sync.dma_start(offs_sb[:], offs)
+        for q in range(4):
+            nc.scalar.dma_start(x_scale_table[32 * q : 32 * q + 4, :].bitcast(I32), x_scales[0, 4 * q : 4 * q + 4, :].bitcast(I32))
+        nc.sync.dma_start(x_table[:].bitcast(I32), x_words[0].rearrange("p n t -> p (n t)").bitcast(I32))
+        nc.sync.dma_start(h_raw[:], hT.rearrange("(p j) i -> p j i", j=PACK))
+        nc.sync.dma_start(wl_sb[:], wl)
+        nc.gpsimd.dma_start(unit_sb[:], unit.rearrange("(p t) o -> p (t o)", t=PACK))
+
+        x_bytes = keep.tile([P, S], U8, name="x_bytes", align_bytes=64)
+        nc.vector.tensor_copy(x_bytes[:], x_scale_table[:].indirect(offs_sb[:]))
+        w_raw = keep.tile([P, PACK, N], F32, name="w_raw", tag="scales_then_w", align_bytes=64)
+        nc.sync.dma_start(w_raw[:], w1.rearrange("(p j) m -> p j m", j=PACK))
+
+        def gather_codes(b, tag):
+            codes = keep.tile([P, BANK], U32, name=f"x_codes{b}", tag=tag, align_bytes=64)
+            nc.vector.tensor_copy(codes[:], x_table[:].indirect(offs_sb[:, b * (BANK // 16) : (b + 1) * (BANK // 16)]))
+            return codes
+
+        x_codes = [gather_codes(0, "x_codes0")]
+
+        h_codes = keep.tile([P, H], U32, name="h_codes", align_bytes=64)
+        h_bytes = keep.tile([P, H], U8, name="h_bytes", align_bytes=64)
+        h_bf = {(c, g): keep.tile([P, 2, P // 2, PACK], BF16, name=f"h_bf{c}{g}", tag=f"h_bf{c}{g}", align_bytes=64) for c in range(2) for g in range(2)}
+        h_dealt = h_raw[:].rearrange("p j (m t) -> p m t j", t=PACK)
+        for g in range(2):
+            for c in range(2):
+                src = h_dealt[:, c * (P // 2) : (c + 1) * (P // 2), 2 * g : 2 * g + 2]
+                dst = h_bf[c, g][:].rearrange("p t m j -> p m t j")
+                if c == 0:
+                    nc.vector.tensor_copy(dst, src)
+                else:
+                    nc.scalar.copy(dst, src)
+        for t in range(PACK):
+            for c in range(2):
+                cols = slice(t * P + c * (P // 2), t * P + (c + 1) * (P // 2))
+                nc.vector.quantize_mx(out=h_codes[:, cols].bitcast(FP8X4), scales=h_bytes[:, cols], in_=h_bf[c, t // 2][:, t % 2].rearrange("p m j -> p (m j)"))
+            if t == 1:
+                x_codes.append(gather_codes(1, "h_bf10"))
+        imp_sb = keep.tile([P, PACK, U], F32, name="imp_sb", tag="table_then_imp", align_bytes=64)
+        nc.sync.dma_start(imp_sb[:], imp.rearrange("(p t) r -> p t r", t=PACK))
+
+        banks = {}
+        for g in range(2):
+            for b in range(2):
+                for t in range(2 * g, 2 * g + 2):
+                    bank = psum.tile([P, BANK], F32, name="bank")
+                    nc.tensor.matmul_mx(
+                        out=bank[:],
+                        lhsT=h_codes[:, t * P : (t + 1) * P].bitcast(FP8X4),
+                        lhsT_scale=h_bytes[:, t * P : (t + 1) * P],
+                        rhs=x_codes[b][:].bitcast(FP8X4),
+                        rhs_scale=x_bytes[:, b * BANK : (b + 1) * BANK],
+                        start=True,
+                        stop=True,
+                    )
+                    banks[t, b] = bank
+
+        odd = [keep.tile([P, 2, V], F32, name=f"odd{t}") for t in range(PACK)]
+        sums = [keep.tile([P, 2, V], F32, name=f"sums{t}") for t in range(PACK)]
+        diffs = [keep.tile([P, 3, V], F32, name=f"diffs{t}") for t in range(PACK)]
+        squares = [keep.tile([P, 3, V], F32, name=f"squares{t}") for t in range(PACK)]
+        pair_var = [keep.tile([P, V], F32, name=f"pair_var{t}") for t in range(PACK)]
+        roots = [keep.tile([P, 2, V], F32, name=f"roots{t}", tag=f"roots{t}") for t in range(PACK)]
+        sd_win = [keep.tile([P, 3 * V], F32, name=f"sd_win{t}") for t in range(PACK)]
+        skw_win = [keep.tile([P, 3 * V], F32, name=f"skw_win{t}") for t in range(PACK)]
+        fetched = {}
+        kw_imp = [keep.tile([P, PACK, HALF], F32, name=f"kw_imp{c}") for c in range(2)]
+
+        def front(t):
+            for b in range(2):
+                groups = slice(b * VB, (b + 1) * VB)
+                members = banks[t, b][:].rearrange("p (v h e) -> p e h v", h=2, e=2)
+                nc.scalar.copy(odd[t][:, :, groups], members[:, 1])
+                nc.vector.tensor_tensor(diffs[t][:, 0:2, groups], members[:, 0], odd[t][:, :, groups], ALU.subtract)
+                nc.vector.tensor_tensor(sums[t][:, :, groups], members[:, 0], odd[t][:, :, groups], ALU.add)
+            nc.scalar.activation(squares[t][:, 0:2], diffs[t][:, 0:2], ACT.Square, scale=0.25)
+            nc.vector.tensor_tensor(diffs[t][:, 2], sums[t][:, 0], sums[t][:, 1], ALU.subtract)
+            nc.scalar.activation(squares[t][:, 2], diffs[t][:, 2], ACT.Square, scale=0.25)
+
+        def middle(t):
+            var = sd_win[t][:, V : 2 * V]
+            nc.vector.scalar_tensor_tensor(pair_var[t][:], squares[t][:, 0], 0.05, squares[t][:, 1], ALU.add, ALU.add)
+            nc.vector.tensor_tensor(skw_win[t][:, 2 * V :], squares[t][:, 0], squares[t][:, 1], ALU.subtract)
+            nc.vector.scalar_tensor_tensor(var, pair_var[t][:], 2.0, squares[t][:, 2], ALU.mult, ALU.add)
+            nc.vector.scalar_tensor_tensor(skw_win[t][:, V : 2 * V], skw_win[t][:, 2 * V :], unit_sb[:, t : t + 1], diffs[t][:, 2], ALU.mult, ALU.mult)
+            nc.scalar.activation(sd_win[t][:, 2 * V :], var, ACT.Square, bias=0.2)
+            nc.scalar.activation(roots[t][:].rearrange("p a v -> p (a v)"), sd_win[t][:, V:], ACT.Abs_reciprocal_sqrt)
+
+        def back(t):
+            nc.vector.scalar_tensor_tensor(sd_win[t][:, 0:V], sd_win[t][:, V : 2 * V], unit_sb[:, t : t + 1], roots[t][:, 0], ALU.mult, ALU.mult)
+            nc.vector.scalar_tensor_tensor(skw_win[t][:, 0:V], skw_win[t][:, V : 2 * V], 1.5, roots[t][:, 1], ALU.mult, ALU.mult)
+
+        def look_up(t, c, fused):
+            cols = slice(c * HALF, (c + 1) * HALF)
+            entries = wl_sb[:, c * (HALF // 16) : (c + 1) * (HALF // 16)]
+            nc.scalar.activation(fetched[c][:, 0, t], sd_win[t][:].indirect(entries), ACT.Copy)
+            if fused:
+                nc.vector.tensor_tensor(kw_imp[c][:, t], skw_win[t][:].indirect(entries), imp_sb[:, t, cols], ALU.mult)
+            else:
+                nc.scalar.activation(fetched[c][:, 1, t], skw_win[t][:].indirect(entries), ACT.Copy)
+                nc.vector.tensor_tensor(kw_imp[c][:, t], fetched[c][:, 1, t], imp_sb[:, t, cols], ALU.mult)
+
+        w_bf = keep.tile([P, N, PACK], BF16, name="w_bf", align_bytes=64)
+        w_codes = keep.tile([P, N], U32, name="w_codes", align_bytes=64)
+        w_bytes = keep.tile([P, N], U8, name="w_bytes", align_bytes=64)
+        hid_bf = [keep.tile([P, HALF, PACK], BF16, name=f"hid_bf{c}", align_bytes=64) for c in range(2)]
+        hid_codes = keep.tile([P, U], U32, name="hid_codes", align_bytes=64)
+        hid_bytes = keep.tile([P, U], U8, name="hid_bytes", align_bytes=64)
+        result = keep.tile([P, 2, 2, HALF], F32, name="result")
+
+        def prepare_w():
+            nc.scalar.copy(w_bf[:].rearrange("p (c i) j -> p c j i", i=2), w_raw[:].rearrange("p j (c i) -> p c j i", i=2))
+            nc.vector.quantize_mx(out=w_codes[:].bitcast(FP8X4), scales=w_bytes[:], in_=w_bf[:].rearrange("p m j -> p (m j)"))
+
+        def finish(c):
+            cols = slice(c * HALF, (c + 1) * HALF)
+            nc.vector.tensor_tensor(
+                hid_bf[c][:].rearrange("p (c i) t -> p c t i", i=2),
+                kw_imp[c][:].rearrange("p t (c i) -> p c t i", i=2),
+                fetched[c][:, 0].rearrange("p t (c i) -> p c t i", i=2),
+                ALU.add,
+            )
+            nc.vector.quantize_mx(out=hid_codes[:, cols].bitcast(FP8X4), scales=hid_bytes[:, cols], in_=hid_bf[c][:].rearrange("p r t -> p (r t)"))
+            for a in range(2):
+                bank = psum.tile([P, BANK], F32, name="bank")
+                nc.tensor.matmul_mx(
+                    out=bank[:, 0:HALF],
+                    lhsT=w_codes[:, a * P : (a + 1) * P].bitcast(FP8X4),
+                    lhsT_scale=w_bytes[:, a * P : (a + 1) * P],
+                    rhs=hid_codes[:, cols].bitcast(FP8X4),
+                    rhs_scale=hid_bytes[:, cols],
+                    start=True,
+                    stop=True,
+                )
+                if a == 0 or c == 0:
+                    nc.scalar.copy(result[:, c, a], bank[:, 0:HALF])
+                else:
+                    nc.vector.tensor_copy(result[:, c, a], bank[:, 0:HALF])
+                nc.sync.dma_start(out[a * P : (a + 1) * P, cols], result[:, c, a])
+
+        prepare_w()
+        for step in range(PACK + 2):
+            if step < PACK:
+                front(step)
+            if 2 <= step:
+                back(step - 2)
+            if 1 <= step <= PACK:
+                middle(step - 1)
+        for c in range(2):
+            fetched[c] = keep.tile([P, 2, PACK, HALF], F32, name=f"fetched{c}", tag=f"roots{PACK - 1}" if c == 1 else "fetched0")
+            for t in range(PACK):
+                look_up(t, c, c == 1 and t >= 2)
+            finish(c)

@@ -33,16 +33,20 @@ def tile_picked_yvladx_lin_p_kernel(tc, x_words, x_scales, hT, imp, unit, w1, of
         x_table = keep.tile([P, T], U32, name="x_table", tag="table_then_imp", align_bytes=64)
         x_scale_table = keep.tile([P, T], U8, name="x_scale_table", tag="scales_then_w", align_bytes=64)
         h_raw = keep.tile([P, PACK, H], F32, name="h_raw")
-        unit_sb = keep.tile([P, PACK], F32, name="unit_sb")
+        one = keep.tile([P, 1], F32, name="one")
+        warm = keep.tile([P, 1], F32, name="warm")
 
         nc.vector.memset(x_scale_table[:].bitcast(I32), 0)
+        x_rows = x_words[0].rearrange("p n t -> p (n t)").bitcast(I32)
         nc.sync.dma_start(offs_sb[:], offs)
-        for q in range(4):
-            nc.scalar.dma_start(x_scale_table[32 * q : 32 * q + 4, :].bitcast(I32), x_scales[0, 4 * q : 4 * q + 4, :].bitcast(I32))
-        nc.sync.dma_start(x_table[:].bitcast(I32), x_words[0].rearrange("p n t -> p (n t)").bitcast(I32))
-        nc.sync.dma_start(h_raw[:], hT.rearrange("(p j) i -> p j i", j=PACK))
+        nc.sync.dma_start(x_table[:, 0 : T // 2].bitcast(I32), x_rows[:, 0 : T // 2])
         nc.sync.dma_start(wl_sb[:], wl)
-        nc.gpsimd.dma_start(unit_sb[:], unit.rearrange("(p t) o -> p (t o)", t=PACK))
+        for q in range(4):
+            nc.sync.dma_start(x_scale_table[32 * q : 32 * q + 4, :].bitcast(I32), x_scales[0, 4 * q : 4 * q + 4, :].bitcast(I32))
+        nc.sync.dma_start(x_table[:, T // 2 :].bitcast(I32), x_rows[:, T // 2 :])
+        nc.sync.dma_start(h_raw[:], hT.rearrange("(p j) i -> p j i", j=PACK))
+        nc.vector.memset(one[:], 1.0)
+        nc.scalar.activation(warm[:], one[:], ACT.Abs_reciprocal_sqrt)
 
         x_bytes = keep.tile([P, S], U8, name="x_bytes", align_bytes=64)
         nc.vector.tensor_copy(x_bytes[:], x_scale_table[:].indirect(offs_sb[:]))
@@ -58,22 +62,17 @@ def tile_picked_yvladx_lin_p_kernel(tc, x_words, x_scales, hT, imp, unit, w1, of
 
         h_codes = keep.tile([P, H], U32, name="h_codes", align_bytes=64)
         h_bytes = keep.tile([P, H], U8, name="h_bytes", align_bytes=64)
-        h_bf = {(c, g): keep.tile([P, 2, P // 2, PACK], BF16, name=f"h_bf{c}{g}", tag=f"h_bf{c}{g}", align_bytes=64) for c in range(2) for g in range(2)}
+        h_bf = [keep.tile([P, 2, P, PACK], BF16, name=f"h_bf{g}", tag=f"h_bf{g}", align_bytes=64) for g in range(2)]
         h_dealt = h_raw[:].rearrange("p j (m t) -> p m t j", t=PACK)
+        nc.vector.tensor_copy(h_bf[0][:].rearrange("p t m j -> p m t j"), h_dealt[:, :, 0:2])
+        nc.scalar.copy(h_bf[1][:].rearrange("p t m j -> p m t j"), h_dealt[:, :, 2:4])
         for g in range(2):
-            for c in range(2):
-                src = h_dealt[:, c * (P // 2) : (c + 1) * (P // 2), 2 * g : 2 * g + 2]
-                dst = h_bf[c, g][:].rearrange("p t m j -> p m t j")
-                if c == 0:
-                    nc.vector.tensor_copy(dst, src)
-                else:
-                    nc.scalar.copy(dst, src)
-        for t in range(PACK):
-            for c in range(2):
-                cols = slice(t * P + c * (P // 2), t * P + (c + 1) * (P // 2))
-                nc.vector.quantize_mx(out=h_codes[:, cols].bitcast(FP8X4), scales=h_bytes[:, cols], in_=h_bf[c, t // 2][:, t % 2].rearrange("p m j -> p (m j)"))
-            if t == 1:
-                x_codes.append(gather_codes(1, "h_bf10"))
+            cols = slice(2 * g * P, 2 * (g + 1) * P)
+            nc.vector.quantize_mx(out=h_codes[:, cols].bitcast(FP8X4), scales=h_bytes[:, cols], in_=h_bf[g][:].rearrange("p t m j -> p (t m j)"))
+            if g == 0:
+                x_codes.append(gather_codes(1, "h_bf0"))
+        unit_sb = keep.tile([P, PACK], F32, name="unit_sb", tag="h_bf1", align_bytes=64)
+        nc.sync.dma_start(unit_sb[:], unit.rearrange("(p t) o -> p (t o)", t=PACK))
         imp_sb = keep.tile([P, PACK, U], F32, name="imp_sb", tag="table_then_imp", align_bytes=64)
         nc.sync.dma_start(imp_sb[:], imp.rearrange("(p t) r -> p t r", t=PACK))
 
@@ -120,61 +119,62 @@ def tile_picked_yvladx_lin_p_kernel(tc, x_words, x_scales, hT, imp, unit, w1, of
             nc.vector.scalar_tensor_tensor(pair_var[t][:], squares[t][:, 0], 0.05, squares[t][:, 1], ALU.add, ALU.add)
             nc.vector.tensor_tensor(skw_win[t][:, 2 * V :], squares[t][:, 0], squares[t][:, 1], ALU.subtract)
             nc.vector.scalar_tensor_tensor(var, pair_var[t][:], 2.0, squares[t][:, 2], ALU.mult, ALU.add)
-            nc.vector.scalar_tensor_tensor(skw_win[t][:, V : 2 * V], skw_win[t][:, 2 * V :], unit_sb[:, t : t + 1], diffs[t][:, 2], ALU.mult, ALU.mult)
-            nc.scalar.activation(sd_win[t][:, 2 * V :], var, ACT.Square, bias=0.2)
+            nc.vector.tensor_tensor(skw_win[t][:, V : 2 * V], skw_win[t][:, 2 * V :], diffs[t][:, 2], ALU.mult)
+            nc.scalar.activation(sd_win[t][:, 2 * V :], var, ACT.Square, scale=1 / 1.5, bias=0.2 / 1.5)
             nc.scalar.activation(roots[t][:].rearrange("p a v -> p (a v)"), sd_win[t][:, V:], ACT.Abs_reciprocal_sqrt)
 
         def back(t):
             nc.vector.scalar_tensor_tensor(sd_win[t][:, 0:V], sd_win[t][:, V : 2 * V], unit_sb[:, t : t + 1], roots[t][:, 0], ALU.mult, ALU.mult)
-            nc.vector.scalar_tensor_tensor(skw_win[t][:, 0:V], skw_win[t][:, V : 2 * V], 1.5, roots[t][:, 1], ALU.mult, ALU.mult)
+            nc.vector.scalar_tensor_tensor(skw_win[t][:, 0:V], skw_win[t][:, V : 2 * V], unit_sb[:, t : t + 1], roots[t][:, 1], ALU.mult, ALU.mult)
 
-        def look_up(t, c, fused):
+        def look_up(c, plain):
             cols = slice(c * HALF, (c + 1) * HALF)
             entries = wl_sb[:, c * (HALF // 16) : (c + 1) * (HALF // 16)]
-            nc.scalar.activation(fetched[c][:, 0, t], sd_win[t][:].indirect(entries), ACT.Copy)
-            if fused:
-                nc.vector.tensor_tensor(kw_imp[c][:, t], skw_win[t][:].indirect(entries), imp_sb[:, t, cols], ALU.mult)
-            else:
+            for t in range(plain):
+                nc.scalar.activation(fetched[c][:, 0, t], sd_win[t][:].indirect(entries), ACT.Copy)
                 nc.scalar.activation(fetched[c][:, 1, t], skw_win[t][:].indirect(entries), ACT.Copy)
-                nc.vector.tensor_tensor(kw_imp[c][:, t], fetched[c][:, 1, t], imp_sb[:, t, cols], ALU.mult)
+            nc.vector.tensor_tensor(kw_imp[c][:, 0:plain], fetched[c][:, 1, 0:plain], imp_sb[:, 0:plain, cols], ALU.mult)
+            for t in range(plain, PACK):
+                nc.scalar.activation(fetched[c][:, 0, t], sd_win[t][:].indirect(entries), ACT.Copy)
+            for t in range(plain, PACK):
+                nc.vector.tensor_tensor(kw_imp[c][:, t], skw_win[t][:].indirect(entries), imp_sb[:, t, cols], ALU.mult)
 
         w_bf = keep.tile([P, N, PACK], BF16, name="w_bf", align_bytes=64)
         w_codes = keep.tile([P, N], U32, name="w_codes", align_bytes=64)
         w_bytes = keep.tile([P, N], U8, name="w_bytes", align_bytes=64)
-        hid_bf = [keep.tile([P, HALF, PACK], BF16, name=f"hid_bf{c}", align_bytes=64) for c in range(2)]
-        hid_codes = keep.tile([P, U], U32, name="hid_codes", align_bytes=64)
-        hid_bytes = keep.tile([P, U], U8, name="hid_bytes", align_bytes=64)
-        result = keep.tile([P, 2, 2, HALF], F32, name="result")
-
         def prepare_w():
             nc.scalar.copy(w_bf[:].rearrange("p (c i) j -> p c j i", i=2), w_raw[:].rearrange("p j (c i) -> p c j i", i=2))
             nc.vector.quantize_mx(out=w_codes[:].bitcast(FP8X4), scales=w_bytes[:], in_=w_bf[:].rearrange("p m j -> p (m j)"))
 
-        def finish(c):
-            cols = slice(c * HALF, (c + 1) * HALF)
+        def finish(c, first, width, last):
+            part = slice(first, first + width)
+            hid_bf = keep.tile([P, width, PACK], BF16, name=f"hid_bf{c}_{first}", align_bytes=64)
+            hid_codes = keep.tile([P, width], U32, name=f"hid_codes{c}_{first}", align_bytes=64)
+            hid_bytes = keep.tile([P, width], U8, name=f"hid_bytes{c}_{first}", align_bytes=64)
             nc.vector.tensor_tensor(
-                hid_bf[c][:].rearrange("p (c i) t -> p c t i", i=2),
-                kw_imp[c][:].rearrange("p t (c i) -> p c t i", i=2),
-                fetched[c][:, 0].rearrange("p t (c i) -> p c t i", i=2),
+                hid_bf[:].rearrange("p (c i) t -> p c t i", i=2),
+                kw_imp[c][:, :, part].rearrange("p t (c i) -> p c t i", i=2),
+                fetched[c][:, 0, :, part].rearrange("p t (c i) -> p c t i", i=2),
                 ALU.add,
             )
-            nc.vector.quantize_mx(out=hid_codes[:, cols].bitcast(FP8X4), scales=hid_bytes[:, cols], in_=hid_bf[c][:].rearrange("p r t -> p (r t)"))
+            nc.vector.quantize_mx(out=hid_codes[:].bitcast(FP8X4), scales=hid_bytes[:], in_=hid_bf[:].rearrange("p r t -> p (r t)"))
             for a in range(2):
                 bank = psum.tile([P, BANK], F32, name="bank")
                 nc.tensor.matmul_mx(
-                    out=bank[:, 0:HALF],
+                    out=bank[:, 0:width],
                     lhsT=w_codes[:, a * P : (a + 1) * P].bitcast(FP8X4),
                     lhsT_scale=w_bytes[:, a * P : (a + 1) * P],
-                    rhs=hid_codes[:, cols].bitcast(FP8X4),
-                    rhs_scale=hid_bytes[:, cols],
+                    rhs=hid_codes[:].bitcast(FP8X4),
+                    rhs_scale=hid_bytes[:],
                     start=True,
                     stop=True,
                 )
-                if a == 0 or c == 0:
-                    nc.scalar.copy(result[:, c, a], bank[:, 0:HALF])
+                result = keep.tile([P, width], F32, name=f"result{c}_{first}_{a}")
+                if a == 1 and last:
+                    nc.vector.tensor_copy(result[:], bank[:, 0:width])
                 else:
-                    nc.vector.tensor_copy(result[:, c, a], bank[:, 0:HALF])
-                nc.sync.dma_start(out[a * P : (a + 1) * P, cols], result[:, c, a])
+                    nc.scalar.copy(result[:], bank[:, 0:width])
+                nc.sync.dma_start(out[a * P : (a + 1) * P, c * HALF + first : c * HALF + first + width], result[:])
 
         prepare_w()
         for step in range(PACK + 2):
@@ -184,8 +184,10 @@ def tile_picked_yvladx_lin_p_kernel(tc, x_words, x_scales, hT, imp, unit, w1, of
                 back(step - 2)
             if 1 <= step <= PACK:
                 middle(step - 1)
-        for c in range(2):
-            fetched[c] = keep.tile([P, 2, PACK, HALF], F32, name=f"fetched{c}", tag=f"roots{PACK - 1}" if c == 1 else "fetched0")
-            for t in range(PACK):
-                look_up(t, c, c == 1 and t >= 2)
-            finish(c)
+        fetched[0] = keep.tile([P, 2, PACK, HALF], F32, name="fetched0")
+        look_up(0, 3)
+        finish(0, 0, HALF, False)
+        fetched[1] = keep.tile([P, 2, PACK, HALF], F32, name="fetched1", tag="roots2")
+        look_up(1, 2)
+        finish(1, 0, HALF // 2, False)
+        finish(1, HALF // 2, HALF // 2, True)

@@ -31,61 +31,58 @@ def tile_picked_yvladx_lin_p_kernel(tc, x_words, x_scales, hT, imp, unit, w1, of
         offs_sb = keep.tile([P, S // 16], U16, name="offs_sb")
         wl_sb = keep.tile([P, U // 16], U16, name="wl_sb")
         x_table = keep.tile([P, T], U32, name="x_table", tag="table_then_imp", align_bytes=64)
-        x_scale_table = keep.tile([P, T], U8, name="x_scale_table", tag="scales_then_w", align_bytes=64)
-        h_raw = keep.tile([P, PACK, H], F32, name="h_raw")
+        x_scale_table = keep.tile([P, T], U8, name="x_scale_table", align_bytes=64)
+        h_raw = [keep.tile([P, PACK, H // 2], F32, name=f"h_raw{c}") for c in range(2)]
+        w_raw = keep.tile([P, PACK, N], F32, name="w_raw")
         one = keep.tile([P, 1], F32, name="one")
         warm = keep.tile([P, 1], F32, name="warm")
 
         nc.vector.memset(x_scale_table[:].bitcast(I32), 0)
         x_rows = x_words[0].rearrange("p n t -> p (n t)").bitcast(I32)
         nc.sync.dma_start(offs_sb[:], offs)
-        nc.sync.dma_start(x_table[:, 0 : T // 2].bitcast(I32), x_rows[:, 0 : T // 2])
+        nc.sync.dma_start(x_table[:, 0 : T // 4].bitcast(I32), x_rows[:, 0 : T // 4])
         nc.sync.dma_start(wl_sb[:], wl)
         for q in range(4):
             nc.sync.dma_start(x_scale_table[32 * q : 32 * q + 4, :].bitcast(I32), x_scales[0, 4 * q : 4 * q + 4, :].bitcast(I32))
-        nc.sync.dma_start(x_table[:, T // 2 :].bitcast(I32), x_rows[:, T // 2 :])
-        nc.sync.dma_start(h_raw[:], hT.rearrange("(p j) i -> p j i", j=PACK))
+        h_rows = hT.rearrange("(p j) i -> p j i", j=PACK)
+        nc.sync.dma_start(x_table[:, T // 4 :].bitcast(I32), x_rows[:, T // 4 :])
+        nc.sync.dma_start(h_raw[0][:], h_rows[:, :, 0 : H // 2])
+        nc.sync.dma_start(h_raw[1][:], h_rows[:, :, H // 2 :])
+        nc.sync.dma_start(w_raw[:], w1.rearrange("(p j) m -> p j m", j=PACK))
         nc.vector.memset(one[:], 1.0)
         nc.scalar.activation(warm[:], one[:], ACT.Abs_reciprocal_sqrt)
 
         x_bytes = keep.tile([P, S], U8, name="x_bytes", align_bytes=64)
         nc.vector.tensor_copy(x_bytes[:], x_scale_table[:].indirect(offs_sb[:]))
-        w_raw = keep.tile([P, PACK, N], F32, name="w_raw", tag="scales_then_w", align_bytes=64)
-        nc.sync.dma_start(w_raw[:], w1.rearrange("(p j) m -> p j m", j=PACK))
-
-        def gather_codes(b, tag):
-            codes = keep.tile([P, BANK], U32, name=f"x_codes{b}", tag=tag, align_bytes=64)
-            nc.vector.tensor_copy(codes[:], x_table[:].indirect(offs_sb[:, b * (BANK // 16) : (b + 1) * (BANK // 16)]))
-            return codes
-
-        x_codes = [gather_codes(0, "x_codes0")]
+        x_codes = keep.tile([P, S], U32, name="x_codes", align_bytes=64)
+        for b in range(2):
+            nc.vector.tensor_copy(x_codes[:, b * BANK : (b + 1) * BANK], x_table[:].indirect(offs_sb[:, b * (BANK // 16) : (b + 1) * (BANK // 16)]))
 
         h_codes = keep.tile([P, H], U32, name="h_codes", align_bytes=64)
         h_bytes = keep.tile([P, H], U8, name="h_bytes", align_bytes=64)
         h_bf = [keep.tile([P, 2, P, PACK], BF16, name=f"h_bf{g}", tag=f"h_bf{g}", align_bytes=64) for g in range(2)]
-        h_dealt = h_raw[:].rearrange("p j (m t) -> p m t j", t=PACK)
-        nc.vector.tensor_copy(h_bf[0][:].rearrange("p t m j -> p m t j"), h_dealt[:, :, 0:2])
-        nc.scalar.copy(h_bf[1][:].rearrange("p t m j -> p m t j"), h_dealt[:, :, 2:4])
+        for c in range(2):
+            h_dealt = h_raw[c][:].rearrange("p j (m t) -> p m t j", t=PACK)
+            for g in range(2):
+                nc.scalar.copy(h_bf[g][:].rearrange("p t m j -> p m t j")[:, c * (P // 2) : (c + 1) * (P // 2)], h_dealt[:, :, 2 * g : 2 * g + 2])
         for g in range(2):
             cols = slice(2 * g * P, 2 * (g + 1) * P)
             nc.vector.quantize_mx(out=h_codes[:, cols].bitcast(FP8X4), scales=h_bytes[:, cols], in_=h_bf[g][:].rearrange("p t m j -> p (t m j)"))
-            if g == 0:
-                x_codes.append(gather_codes(1, "h_bf0"))
         unit_sb = keep.tile([P, PACK], F32, name="unit_sb", tag="h_bf1", align_bytes=64)
         nc.sync.dma_start(unit_sb[:], unit.rearrange("(p t) o -> p (t o)", t=PACK))
         imp_sb = keep.tile([P, PACK, U], F32, name="imp_sb", tag="table_then_imp", align_bytes=64)
         nc.sync.dma_start(imp_sb[:], imp.rearrange("(p t) r -> p t r", t=PACK))
 
         banks = {}
-        for g in range(2):
+        for t in range(PACK):
             for b in range(2):
-                for t in range(2 * g, 2 * g + 2):
+                if True:
                     bank = psum.tile([P, BANK], F32, name="bank")
                     nc.tensor.matmul_mx(
                         out=bank[:],
                         lhsT=h_codes[:, t * P : (t + 1) * P].bitcast(FP8X4),
                         lhsT_scale=h_bytes[:, t * P : (t + 1) * P],
-                        rhs=x_codes[b][:].bitcast(FP8X4),
+                        rhs=x_codes[:, b * BANK : (b + 1) * BANK].bitcast(FP8X4),
                         rhs_scale=x_bytes[:, b * BANK : (b + 1) * BANK],
                         start=True,
                         stop=True,
@@ -143,10 +140,10 @@ def tile_picked_yvladx_lin_p_kernel(tc, x_words, x_scales, hT, imp, unit, w1, of
         w_codes = keep.tile([P, N], U32, name="w_codes", align_bytes=64)
         w_bytes = keep.tile([P, N], U8, name="w_bytes", align_bytes=64)
         def prepare_w():
-            nc.scalar.copy(w_bf[:].rearrange("p (c i) j -> p c j i", i=2), w_raw[:].rearrange("p j (c i) -> p c j i", i=2))
+            nc.vector.tensor_copy(w_bf[:].rearrange("p (c i) j -> p c j i", i=2), w_raw[:].rearrange("p j (c i) -> p c j i", i=2))
             nc.vector.quantize_mx(out=w_codes[:].bitcast(FP8X4), scales=w_bytes[:], in_=w_bf[:].rearrange("p m j -> p (m j)"))
 
-        def finish(c, first, width, last):
+        def finish(c, first, width):
             part = slice(first, first + width)
             hid_bf = keep.tile([P, width, PACK], BF16, name=f"hid_bf{c}_{first}", align_bytes=64)
             hid_codes = keep.tile([P, width], U32, name=f"hid_codes{c}_{first}", align_bytes=64)
@@ -158,10 +155,10 @@ def tile_picked_yvladx_lin_p_kernel(tc, x_words, x_scales, hT, imp, unit, w1, of
                 ALU.add,
             )
             nc.vector.quantize_mx(out=hid_codes[:].bitcast(FP8X4), scales=hid_bytes[:], in_=hid_bf[:].rearrange("p r t -> p (r t)"))
+            bank = psum.tile([P, BANK], F32, name="bank")
             for a in range(2):
-                bank = psum.tile([P, BANK], F32, name="bank")
                 nc.tensor.matmul_mx(
-                    out=bank[:, 0:width],
+                    out=bank[:, a * width : (a + 1) * width],
                     lhsT=w_codes[:, a * P : (a + 1) * P].bitcast(FP8X4),
                     lhsT_scale=w_bytes[:, a * P : (a + 1) * P],
                     rhs=hid_codes[:].bitcast(FP8X4),
@@ -169,12 +166,9 @@ def tile_picked_yvladx_lin_p_kernel(tc, x_words, x_scales, hT, imp, unit, w1, of
                     start=True,
                     stop=True,
                 )
-                result = keep.tile([P, width], F32, name=f"result{c}_{first}_{a}")
-                if a == 1 and last:
-                    nc.vector.tensor_copy(result[:], bank[:, 0:width])
-                else:
-                    nc.scalar.copy(result[:], bank[:, 0:width])
-                nc.sync.dma_start(out[a * P : (a + 1) * P, c * HALF + first : c * HALF + first + width], result[:])
+            result = keep.tile([P, 2, width], F32, name=f"result{c}_{first}")
+            nc.scalar.copy(result[:].rearrange("p a r -> p (a r)"), bank[:, 0 : 2 * width])
+            nc.sync.dma_start(out.rearrange("(a p) r -> p a r", a=2)[:, :, c * HALF + first : c * HALF + first + width], result[:])
 
         prepare_w()
         for step in range(PACK + 2):
@@ -186,8 +180,8 @@ def tile_picked_yvladx_lin_p_kernel(tc, x_words, x_scales, hT, imp, unit, w1, of
                 middle(step - 1)
         fetched[0] = keep.tile([P, 2, PACK, HALF], F32, name="fetched0")
         look_up(0, 3)
-        finish(0, 0, HALF, False)
+        finish(0, 0, HALF)
         fetched[1] = keep.tile([P, 2, PACK, HALF], F32, name="fetched1", tag="roots2")
-        look_up(1, 2)
-        finish(1, 0, HALF // 2, False)
-        finish(1, HALF // 2, HALF // 2, True)
+        look_up(1, 1)
+        finish(1, 0, HALF // 2)
+        finish(1, HALF // 2, HALF // 2)

from contextlib import ExitStack

import concourse.mybir as mybir

K, T, S, D, N, H, V, U = 512, 2048, 1024, 4, 256, 512, 256, 512
FLOPS = 2 * K * H * S + 2 * H * N * U

F32 = mybir.dt.float32
BF16 = mybir.dt.bfloat16
I32 = mybir.dt.int32
U32 = mybir.dt.uint32
U16 = mybir.dt.uint16
U8 = mybir.dt.uint8
FP8X4 = mybir.dt.float8_e4m3fn_x4
ALU = mybir.AluOpType
ACT = mybir.ActivationFunctionType

P = 128
PACK = 4
BANK = 512
VB = BANK // D
HALF = U // 2


def tile_picked_yvladx_lin_p_kernel(tc, x_words, x_scales, hT, imp, unit, w1, offs, wl, out):
    nc = tc.nc
    with ExitStack() as ctx:
        keep = ctx.enter_context(tc.tile_pool(name="keep", bufs=1))
        psum = ctx.enter_context(tc.psum_pool(name="psum", bufs=8))

        offs_sb = keep.tile([P, S // 16], U16, name="offs_sb")
        wl_sb = keep.tile([P, U // 16], U16, name="wl_sb")
        x_table = keep.tile([P, T], U32, name="x_table", tag="table_then_imp", align_bytes=64)
        x_scale_table = keep.tile([P, T], U8, name="x_scale_table", align_bytes=64)
        h_raw = [keep.tile([P, PACK, H // 2], F32, name=f"h_raw{c}") for c in range(2)]
        w_raw = keep.tile([P, PACK, N], F32, name="w_raw")
        one = keep.tile([P, 1], F32, name="one")
        warm = keep.tile([P, 1], F32, name="warm")

        nc.vector.memset(x_scale_table[:].bitcast(I32), 0)
        x_rows = x_words[0].rearrange("p n t -> p (n t)").bitcast(I32)
        nc.sync.dma_start(offs_sb[:], offs)
        nc.sync.dma_start(x_table[:, 0 : T // 4].bitcast(I32), x_rows[:, 0 : T // 4])
        nc.sync.dma_start(wl_sb[:], wl)
        for q in range(4):
            nc.sync.dma_start(x_scale_table[32 * q : 32 * q + 4, :].bitcast(I32), x_scales[0, 4 * q : 4 * q + 4, :].bitcast(I32))
        h_rows = hT.rearrange("(p j) i -> p j i", j=PACK)
        nc.sync.dma_start(x_table[:, T // 4 :].bitcast(I32), x_rows[:, T // 4 :])
        nc.sync.dma_start(h_raw[0][:], h_rows[:, :, 0 : H // 2])
        nc.sync.dma_start(h_raw[1][:], h_rows[:, :, H // 2 :])
        nc.sync.dma_start(w_raw[:], w1.rearrange("(p j) m -> p j m", j=PACK))
        nc.vector.memset(one[:], 1.0)
        nc.scalar.activation(warm[:], one[:], ACT.Abs_reciprocal_sqrt)

        x_bytes = keep.tile([P, S], U8, name="x_bytes", align_bytes=64)
        nc.vector.tensor_copy(x_bytes[:], x_scale_table[:].indirect(offs_sb[:]))
        x_codes = keep.tile([P, S], U32, name="x_codes", align_bytes=64)
        for b in range(2):
            nc.vector.tensor_copy(x_codes[:, b * BANK : (b + 1) * BANK], x_table[:].indirect(offs_sb[:, b * (BANK // 16) : (b + 1) * (BANK // 16)]))

        h_codes = keep.tile([P, H], U32, name="h_codes", align_bytes=64)
        h_bytes = keep.tile([P, H], U8, name="h_bytes", align_bytes=64)
        h_bf = [keep.tile([P, 2, P, PACK], BF16, name=f"h_bf{g}", tag=f"h_bf{g}", align_bytes=64) for g in range(2)]
        for c in range(2):
            h_dealt = h_raw[c][:].rearrange("p j (m t) -> p m t j", t=PACK)
            for g in range(2):
                nc.scalar.copy(h_bf[g][:].rearrange("p t m j -> p m t j")[:, c * (P // 2) : (c + 1) * (P // 2)], h_dealt[:, :, 2 * g : 2 * g + 2])
        for g in range(2):
            cols = slice(2 * g * P, 2 * (g + 1) * P)
            nc.vector.quantize_mx(out=h_codes[:, cols].bitcast(FP8X4), scales=h_bytes[:, cols], in_=h_bf[g][:].rearrange("p t m j -> p (t m j)"))
        unit_sb = keep.tile([P, PACK], F32, name="unit_sb", tag="h_bf1", align_bytes=64)
        nc.sync.dma_start(unit_sb[:], unit.rearrange("(p t) o -> p (t o)", t=PACK))
        imp_sb = keep.tile([P, PACK, U], F32, name="imp_sb", tag="table_then_imp", align_bytes=64)
        nc.sync.dma_start(imp_sb[:], imp.rearrange("(p t) r -> p t r", t=PACK))

        banks = {}
        for t in range(PACK):
            for b in range(2):
                if True:
                    bank = psum.tile([P, BANK], F32, name="bank")
                    nc.tensor.matmul_mx(
                        out=bank[:],
                        lhsT=h_codes[:, t * P : (t + 1) * P].bitcast(FP8X4),
                        lhsT_scale=h_bytes[:, t * P : (t + 1) * P],
                        rhs=x_codes[:, b * BANK : (b + 1) * BANK].bitcast(FP8X4),
                        rhs_scale=x_bytes[:, b * BANK : (b + 1) * BANK],
                        start=True,
                        stop=True,
                    )
                    banks[t, b] = bank

        odd = [keep.tile([P, 2, V], F32, name=f"odd{t}") for t in range(PACK)]
        sums = [keep.tile([P, 2, V], F32, name=f"sums{t}") for t in range(PACK)]
        diffs = [keep.tile([P, 3, V], F32, name=f"diffs{t}") for t in range(PACK)]
        squares = [keep.tile([P, 3, V], F32, name=f"squares{t}") for t in range(PACK)]
        pair_var = [keep.tile([P, V], F32, name=f"pair_var{t}") for t in range(PACK)]
        roots = [keep.tile([P, 2, V], F32, name=f"roots{t}", tag=f"roots{t}") for t in range(PACK)]
        sd_win = [keep.tile([P, 3 * V], F32, name=f"sd_win{t}") for t in range(PACK)]
        skw_win = [keep.tile([P, 3 * V], F32, name=f"skw_win{t}") for t in range(PACK)]
        fetched = {}
        kw_imp = [keep.tile([P, PACK, HALF], F32, name=f"kw_imp{c}") for c in range(2)]

        def front(t):
            for b in range(2):
                groups = slice(b * VB, (b + 1) * VB)
                members = banks[t, b][:].rearrange("p (v h e) -> p e h v", h=2, e=2)
                nc.scalar.copy(odd[t][:, :, groups], members[:, 1])
                nc.vector.tensor_tensor(diffs[t][:, 0:2, groups], members[:, 0], odd[t][:, :, groups], ALU.subtract)
                nc.vector.tensor_tensor(sums[t][:, :, groups], members[:, 0], odd[t][:, :, groups], ALU.add)
            nc.scalar.activation(squares[t][:, 0:2], diffs[t][:, 0:2], ACT.Square, scale=0.25)
            nc.vector.tensor_tensor(diffs[t][:, 2], sums[t][:, 0], sums[t][:, 1], ALU.subtract)
            nc.scalar.activation(squares[t][:, 2], diffs[t][:, 2], ACT.Square, scale=0.25)

        def middle(t):
            var = sd_win[t][:, V : 2 * V]
            nc.vector.scalar_tensor_tensor(pair_var[t][:], squares[t][:, 0], 0.05, squares[t][:, 1], ALU.add, ALU.add)
            nc.vector.tensor_tensor(skw_win[t][:, 2 * V :], squares[t][:, 0], squares[t][:, 1], ALU.subtract)
            nc.vector.scalar_tensor_tensor(var, pair_var[t][:], 2.0, squares[t][:, 2], ALU.mult, ALU.add)
            nc.vector.tensor_tensor(skw_win[t][:, V : 2 * V], skw_win[t][:, 2 * V :], diffs[t][:, 2], ALU.mult)
            nc.scalar.activation(sd_win[t][:, 2 * V :], var, ACT.Square, scale=1 / 1.5, bias=0.2 / 1.5)
            nc.scalar.activation(roots[t][:].rearrange("p a v -> p (a v)"), sd_win[t][:, V:], ACT.Abs_reciprocal_sqrt)

        def back(t):
            nc.vector.scalar_tensor_tensor(sd_win[t][:, 0:V], sd_win[t][:, V : 2 * V], unit_sb[:, t : t + 1], roots[t][:, 0], ALU.mult, ALU.mult)
            nc.vector.scalar_tensor_tensor(skw_win[t][:, 0:V], skw_win[t][:, V : 2 * V], unit_sb[:, t : t + 1], roots[t][:, 1], ALU.mult, ALU.mult)

        def look_up(c, plain):
            cols = slice(c * HALF, (c + 1) * HALF)
            entries = wl_sb[:, c * (HALF // 16) : (c + 1) * (HALF // 16)]
            for t in range(plain):
                nc.scalar.activation(fetched[c][:, 0, t], sd_win[t][:].indirect(entries), ACT.Copy)
                nc.scalar.activation(fetched[c][:, 1, t], skw_win[t][:].indirect(entries), ACT.Copy)
            nc.vector.tensor_tensor(kw_imp[c][:, 0:plain], fetched[c][:, 1, 0:plain], imp_sb[:, 0:plain, cols], ALU.mult)
            for t in range(plain, PACK):
                nc.scalar.activation(fetched[c][:, 0, t], sd_win[t][:].indirect(entries), ACT.Copy)
            for t in range(plain, PACK):
                nc.vector.tensor_tensor(kw_imp[c][:, t], skw_win[t][:].indirect(entries), imp_sb[:, t, cols], ALU.mult)

        w_bf = keep.tile([P, N, PACK], BF16, name="w_bf", align_bytes=64)
        w_codes = keep.tile([P, N], U32, name="w_codes", align_bytes=64)
        w_bytes = keep.tile([P, N], U8, name="w_bytes", align_bytes=64)
        def prepare_w():
            nc.vector.tensor_copy(w_bf[:].rearrange("p (c i) j -> p c j i", i=2), w_raw[:].rearrange("p j (c i) -> p c j i", i=2))
            nc.vector.quantize_mx(out=w_codes[:].bitcast(FP8X4), scales=w_bytes[:], in_=w_bf[:].rearrange("p m j -> p (m j)"))

        def finish(c, first, width):
            part = slice(first, first + width)
            hid_bf = keep.tile([P, width, PACK], BF16, name=f"hid_bf{c}_{first}", align_bytes=64)
            hid_codes = keep.tile([P, width], U32, name=f"hid_codes{c}_{first}", align_bytes=64)
            hid_bytes = keep.tile([P, width], U8, name=f"hid_bytes{c}_{first}", align_bytes=64)
            nc.vector.tensor_tensor(
                hid_bf[:].rearrange("p (c i) t -> p c t i", i=2),
                kw_imp[c][:, :, part].rearrange("p t (c i) -> p c t i", i=2),
                fetched[c][:, 0, :, part].rearrange("p t (c i) -> p c t i", i=2),
                ALU.add,
            )
            nc.vector.quantize_mx(out=hid_codes[:].bitcast(FP8X4), scales=hid_bytes[:], in_=hid_bf[:].rearrange("p r t -> p (r t)"))
            bank = psum.tile([P, BANK], F32, name="bank")
            for a in range(2):
                nc.tensor.matmul_mx(
                    out=bank[:, a * width : (a + 1) * width],
                    lhsT=w_codes[:, a * P : (a + 1) * P].bitcast(FP8X4),
                    lhsT_scale=w_bytes[:, a * P : (a + 1) * P],
                    rhs=hid_codes[:].bitcast(FP8X4),
                    rhs_scale=hid_bytes[:],
                    start=True,
                    stop=True,
                )
            result = keep.tile([P, 2, width], F32, name=f"result{c}_{first}")
            nc.scalar.copy(result[:].rearrange("p a r -> p (a r)"), bank[:, 0 : 2 * width])
            nc.sync.dma_start(out.rearrange("(a p) r -> p a r", a=2)[:, :, c * HALF + first : c * HALF + first + width], result[:])

        prepare_w()
        for step in range(PACK + 2):
            if step < PACK:
                front(step)
            if 2 <= step:
                back(step - 2)
            if 1 <= step <= PACK:
                middle(step - 1)
        fetched[0] = keep.tile([P, 2, PACK, HALF], F32, name="fetched0")
        look_up(0, 3)
        finish(0, 0, HALF)
        fetched[1] = keep.tile([P, 2, PACK, HALF], F32, name="fetched1", tag="roots2")
        look_up(1, 1)
        finish(1, 0, HALF // 2)
        finish(1, HALF // 2, HALF // 2)
